import numpy as np
import ml_dtypes


def mxq(x, axis, fmt="e4m3"):
    dtype, down = {"e4m3": (ml_dtypes.float8_e4m3fn, 7), "e5m2": (ml_dtypes.float8_e5m2, 14)}[fmt]
    v = np.moveaxis(np.asarray(x, np.float32).astype(ml_dtypes.bfloat16).astype(np.float64), axis, -1)
    blocks = v.reshape(v.shape[:-1] + (-1, 32))
    amax = np.abs(blocks).max(-1, keepdims=True)
    byte = np.maximum(np.where(amax > 0, np.frexp(amax)[1] - 1 + 127, 0) - down, 1)
    scale = np.exp2(byte - 127.0)
    codes = (blocks / scale).astype(np.float32).astype(dtype).astype(np.float64)
    return np.moveaxis((codes * scale).reshape(v.shape), -1, axis)


WIDE = False


def mx_kscale(k):
    if not WIDE:
        return np.ones(k)
    levels = np.array([10, -10, 5, -5, 0])
    if k % 512:
        return np.exp2(np.random.permutation(np.resize(levels, k // 32))).repeat(32)
    a = np.empty((k // 512, 16))
    for p in range(k // 512):
        a[p, :8] = np.random.permutation(np.resize(levels, 8))
        for g in range(8):
            far = levels[np.abs(levels - a[p, g]) >= 10]
            a[p, g + 8] = far[np.random.randint(len(far))]
    return np.exp2(a.ravel()).repeat(32)


def f64(x):
    return np.asarray(x).astype(np.float64)


def striped(idx):
    return np.tile(idx.reshape(-1, 16).T, (8, 1)).astype(np.uint16)


def unstriped(offs):
    return offs[:16].T.reshape(-1).astype(np.int64)


E2M1 = np.array([0.0, 0.5, 1.0, 1.5, 2.0, 3.0, 4.0, 6.0, -0.0, -0.5, -1.0, -1.5, -2.0, -3.0, -4.0, -6.0])


def pack_weight(w, fmt):
    k, n = w.shape
    w = f64(np.asarray(w, np.float32).astype(ml_dtypes.bfloat16)).reshape(k // 32, 32, n)
    amax = np.abs(w).max(1)
    if fmt == "e4m3":
        byte = np.frexp(amax)[1] - 1 + 127 - 7
    else:
        mant, ex = np.frexp(amax / 6.0)
        byte = np.where(mant > 0.5, ex, ex - 1) + 127
    byte = np.clip(np.where(amax > 0, byte, 1), 1, 254)
    scaled = (w * np.exp2(127.0 - byte)[:, None, :]).reshape(k, n).astype(np.float32)
    by_word = np.ascontiguousarray(scaled.reshape(k // 512, 128, 4, n).transpose(0, 1, 3, 2))
    if fmt == "e4m3":
        words = by_word.astype(ml_dtypes.float8_e4m3fn).view(np.uint8)
    else:
        c = by_word.astype(ml_dtypes.float4_e2m1fn).view(np.uint8) & 0xF
        words = (c[..., 0::2] | (c[..., 1::2] << 4)).reshape(k // 512, 128, 2 * n)
    return np.ascontiguousarray(words), np.ascontiguousarray(byte.astype(np.uint8).reshape(k // 512, 16, n))


def unpack_weight(words, scales, fmt):
    g, _, n = scales.shape
    words = np.ascontiguousarray(words).reshape(g, 128, n, -1)
    if fmt == "e4m3":
        vals = words.view(ml_dtypes.float8_e4m3fn).astype(np.float64)
    else:
        nib = np.empty((g, 128, n, 4), np.uint8)
        nib[..., 0::2] = words & 0xF
        nib[..., 1::2] = words >> 4
        vals = E2M1[nib]
    vals = vals * np.repeat(np.exp2(scales.astype(np.float64) - 127.0), 8, axis=1)[..., None]
    return vals.transpose(0, 1, 3, 2).reshape(g * 512, n)


def gelu(v):
    return 0.5 * v * (1.0 + np.tanh(np.sqrt(2.0 / np.pi) * (v + 0.044715 * v**3)))


def striped8(idx):
    return np.concatenate([v.reshape(-1, 16).T for v in idx]).astype(np.uint16)


def unstriped8(offs):
    return np.stack([offs[16 * g:16 * g + 16].T.reshape(-1) for g in range(8)]).astype(np.int64)


def runs(v, idx8):
    k = np.arange(v.shape[0])
    return v[k[:, None], idx8[k % 512 // 64]]


K, K2, H, N, T, S, T2 = 1024, 512, 1024, 512, 2048, 1024, 2048

def setup_inputs():
    n = np.random.standard_normal
    s, s2, u = mx_kscale(K)[:, None], mx_kscale(K2)[:, None], mx_kscale(H)[:, None]
    tab_words, tab_scales = pack_weight(n((K, T)) * s, "e4m3")
    tab2_words, tab2_scales = pack_weight(n((K2, T)) * s2, "e4m3")
    w2_words, w2_scales = pack_weight(0.53 * n((K2, H)) / np.sqrt(K2) / s2, "e2m1")
    w4_words, w4_scales = pack_weight(n((H, N)) / np.sqrt(H) / u, "e4m3")
    return {
        "tab_words": tab_words, "tab_scales": tab_scales,
        "tab2_words": tab2_words, "tab2_scales": tab2_scales,
        "offs": striped8(np.stack([np.random.permutation(T)[:S] for _ in range(8)])),
        "offs2": striped(np.random.permutation(T)[:S]),
        "offs3": striped(np.random.permutation(T2)[:S]),
        "w1": (0.53 * n((K, H)) / np.sqrt(K) / s).astype(np.float32),
        "w2_words": w2_words, "w2_scales": w2_scales,
        "gain": (2.0 * np.exp(0.3 * n(H)) * u[:, 0]).astype(np.float32),
        "w3": (n((H, N)) / np.sqrt(H) / u).astype(np.float32),
        "w4_words": w4_words, "w4_scales": w4_scales,
        "b4": (0.5 * n(N)).astype(np.float32),
        "page1": n((N, T2)).astype(np.float32),
        "wgo": np.exp(0.3 * n((128, S))).astype(np.float32),
    }

def reference(tab_words, tab_scales, tab2_words, tab2_scales, offs, offs2, offs3, w1, w2_words, w2_scales,
              gain, w3, w4_words, w4_scales, b4, page1, wgo):
    v = runs(unpack_weight(tab_words, tab_scales, "e4m3"), unstriped8(offs))
    v2 = unpack_weight(tab2_words, tab2_scales, "e4m3")[:, unstriped(offs2)]
    rig = mxq(f64(w1), 0, "e4m3").T @ v
    mood = unpack_weight(w2_words, w2_scales, "e2m1").T @ v2
    h = np.sin(rig) * np.cos(mood) * f64(gain)[:, None]
    hq = mxq(h, 0, "e4m3")
    ya = mxq(f64(w3), 0, "e4m3").T @ hq
    yb = unpack_weight(w4_words, w4_scales, "e4m3").T @ hq
    y = np.maximum(ya, yb + f64(b4)[:, None])
    out = f64(page1).copy()
    out[:, unstriped(offs3)] = np.tile(f64(wgo), (N // 128, 1)) * y
    return out

@@ -1,0 +1,306 @@
+import math
+from contextlib import ExitStack
+
+import concourse.mybir as mybir
+
+K, K2, H, N, T, S, T2 = 1024, 512, 1024, 512, 2048, 1024, 2048
+FLOPS = 2 * S * (K * H + K2 * H + 2 * H * N)
+
+F32 = mybir.dt.float32
+BF16 = mybir.dt.bfloat16
+I32 = mybir.dt.int32
+U32 = mybir.dt.uint32
+U16 = mybir.dt.uint16
+U8 = mybir.dt.uint8
+FP8X4 = mybir.dt.float8_e4m3fn_x4
+FP4X4 = mybir.dt.float4_e2m1fn_x4
+ACT = mybir.ActivationFunctionType
+ALU = mybir.AluOpType
+
+P = 128
+PACK = 4
+PASS = P * PACK
+CHUNK = 256
+HALF = 512
+LIST_ROWS = 16
+
+
+def tile_list_cue_look_proposer_kernel(
+    tc, tab_words, tab_scales, tab2_words, tab2_scales, offs, offs2, offs3, w1, w2_words, w2_scales,
+    gain, w3, w4_words, w4_scales, b4, page1, wgo, out,
+):
+    nc = tc.nc
+    k_passes = K // PASS
+    r_passes = H // PASS
+    n_tiles = N // P
+    chunks = S // CHUNK
+    halves = S // HALF
+
+    def words_view(dram_words):
+        return dram_words.rearrange("p t i -> p (t i)").bitcast(I32)
+
+    def round_to_bf16(engine, dst, src):
+        if engine == "vector":
+            nc.vector.tensor_copy(out=dst, in_=src)
+        elif engine == "scalar":
+            nc.scalar.activation(out=dst, in_=src, func=ACT.Copy)
+        else:
+            nc.gpsimd.tensor_scalar(out=dst, in0=src, scalar1=1.0, scalar2=0.0, op0=ALU.mult, op1=ALU.add)
+
+    with ExitStack() as ctx:
+        keep = ctx.enter_context(tc.tile_pool(name="keep", bufs=1))
+        work = ctx.enter_context(tc.tile_pool(name="work", bufs=2))
+        psum = ctx.enter_context(tc.psum_pool(name="psum", bufs=2))
+
+        def held(name, shape, dtype):
+            return keep.tile(shape, dtype, name=name, align_bytes=64)
+
+        offs_t = held("offs_t", [P, S // LIST_ROWS], U16)
+        offs2_t = held("offs2_t", [P, S // LIST_ROWS], U16)
+        offs3_t = held("offs3_t", [P, S // LIST_ROWS], U16)
+        tab_w = [held("tab_w%d" % a, [P, T], U32) for a in range(k_passes)]
+        tab_s = held("tab_s", [P, T], U8)
+        tab2_w = held("tab2_w", [P, T], U32)
+        tab2_s = held("tab2_s", [P, T], U8)
+        w2_raw = held("w2_raw", [P, 2 * H], U8)
+        w2_raw_s = held("w2_raw_s", [P, H], U8)
+        w4_w = held("w4_w", [P, r_passes, N], U32)
+        w4_s = held("w4_s", [P, r_passes * N], U8)
+        w1_raw = [[held("w1_raw%d%d" % (b, a), [P, PACK, PASS], F32) for a in range(k_passes)] for b in range(r_passes)]
+        w3_raw = [held("w3_raw%d" % b, [P, PACK, N], F32) for b in range(r_passes)]
+        gain_t = held("gain_t", [P, r_passes, PACK], F32)
+        b4_t = held("b4_t", [P, n_tiles], F32)
+        wgo_t = held("wgo_t", [P, S], F32)
+        pages = [held("page%d" % n, [P, T2], F32) for n in range(n_tiles)]
+
+        for plane in (tab_s, w4_s):
+            nc.vector.memset(plane[:].bitcast(I32), 0)
+
+        def load_quadrant(plane, rows, q):
+            nc.sync.dma_start(
+                plane[32 * q : 32 * (q + 1), :].bitcast(I32),
+                rows[4 * q : 4 * q + 4, :].bitcast(I32).partition_broadcast(8),
+            )
+
+        nc.sync.dma_start(offs2_t[:], offs2)
+        for q in range(4):
+            load_quadrant(tab2_s, tab2_scales[0], q)
+        nc.sync.dma_start(tab2_w[:].bitcast(I32), words_view(tab2_words[0]))
+        nc.sync.dma_start(w2_raw[:].bitcast(I32), w2_words[0].bitcast(I32))
+        for q in range(4):
+            load_quadrant(w2_raw_s, w2_scales[0], q)
+        nc.sync.dma_start(offs_t[:], offs)
+        nc.sync.dma_start(tab_w[0][:].bitcast(I32), words_view(tab_words[0]))
+        for a in range(k_passes):
+            for r in range(2):
+                nc.sync.dma_start(tab_s[4 * a + r : P : 16, :].bitcast(I32), tab_scales[a, r:16:2, :].bitcast(I32))
+        nc.sync.dma_start(gain_t[:], gain.rearrange("(b p t) -> p b t", p=P, t=PACK))
+        nc.sync.dma_start(tab_w[1][:].bitcast(I32), words_view(tab_words[1]))
+        for b in range(r_passes):
+            for a in range(k_passes):
+                nc.sync.dma_start(
+                    w1_raw[b][a][:],
+                    w1[a * PASS : (a + 1) * PASS, b * PASS : (b + 1) * PASS].rearrange("(p j) c -> p j c", j=PACK),
+                )
+        for b in range(r_passes):
+            nc.sync.dma_start(w3_raw[b][:], w3[b * PASS : (b + 1) * PASS, :].rearrange("(p j) c -> p j c", j=PACK))
+        nc.sync.dma_start(w4_w[:].bitcast(I32), w4_words.rearrange("a p c i -> p a (c i)").bitcast(I32))
+        for q in range(4):
+            nc.sync.dma_start(
+                w4_s[32 * q : 32 * q + 4, :].bitcast(I32).rearrange("p (a c) -> p a c", a=r_passes),
+                w4_scales[:, 4 * q : 4 * q + 4, :].bitcast(I32).rearrange("a q c -> q a c"),
+            )
+        with nc.allow_non_contiguous_dma(reason="one bias value a partition"):
+            nc.sync.dma_start(b4_t[:], b4.rearrange("(n p) -> p n", p=P))
+        nc.sync.dma_start(offs3_t[:], offs3)
+        nc.sync.dma_start(wgo_t[:], wgo)
+        for n in range(n_tiles):
+            nc.sync.dma_start(pages[n][:], page1[n * P : (n + 1) * P, :])
+
+        def list_cols(first, count):
+            return slice(first // LIST_ROWS, (first + count) // LIST_ROWS)
+
+        v2_s = held("v2_s", [P, S], U8)
+        v2_w = [held("v2_w%d" % u, [P, HALF], U32) for u in range(halves)]
+        w2_w = held("w2_w", [P, 2 * H], U8)
+        w2_s = held("w2_s", [P, H], U8)
+        nc.vector.tensor_copy(v2_s[:], tab2_s[:].indirect(offs2_t[:]))
+        nc.vector.tensor_copy(v2_w[0][:], tab2_w[:].indirect(offs2_t[:, list_cols(0, HALF)]))
+        nc.vector.tensor_copy(
+            out=w2_w[:].bitcast(U16).rearrange("p (b t m) -> p b m t", b=r_passes, t=PACK),
+            in_=w2_raw[:].bitcast(U16).rearrange("p (b m t) -> p b m t", b=r_passes, t=PACK),
+        )
+        nc.vector.tensor_copy(
+            out=w2_s[:].rearrange("p (b t m) -> p b m t", b=r_passes, t=PACK),
+            in_=w2_raw_s[:].rearrange("p (b m t) -> p b m t", b=r_passes, t=PACK),
+        )
+
+        v_gs = held("v_gs", [P, S], U8)
+        v_s = held("v_s", [P, S], U8)
+        v_w = [[held("v_w%d%d" % (u, a), [P, HALF], U32) for a in range(k_passes)] for u in range(halves)]
+        nc.vector.tensor_copy(v_gs[:], tab_s[:].indirect(offs_t[:]))
+        nc.vector.tensor_copy(out=v_s[:].bitcast(I32), in_=v_gs[:].bitcast(I32))
+        for a in range(k_passes):
+            for r in range(2):
+                nc.gpsimd.dma_start(v_s[4 * a + 2 + r : P : 32, :].bitcast(I32), v_gs[16 + 4 * a + r : P : 32, :].bitcast(I32))
+        for a in range(k_passes):
+            nc.vector.tensor_copy(v_w[0][a][:], tab_w[a][:].indirect(offs_t[:, list_cols(0, HALF)]))
+
+        cos_mood = [[held("cos%d%d" % (u, b), [P, PACK, HALF], F32) for b in range(r_passes)] for u in range(halves)]
+
+        def mood(u, b):
+            size = cos_mood[u][b]
+            for t in range(PACK):
+                col = b * PASS + t * P
+                bank = psum.tile([P, HALF], F32, name="mood_bank")
+                nc.tensor.matmul_mx(
+                    out=bank[:],
+                    lhsT=w2_w[:, 2 * col : 2 * (col + P)].bitcast(FP4X4),
+                    lhsT_scale=w2_s[:, col : col + P],
+                    rhs=v2_w[u][:].bitcast(FP8X4),
+                    rhs_scale=v2_s[:, u * HALF : (u + 1) * HALF],
+                    start=True,
+                    stop=True,
+                )
+                nc.scalar.activation(out=size[:, t, :], in_=bank[:], func=ACT.Abs)
+                if t % 2 == 1:
+                    both = size[:, t - 1 : t + 1, :]
+                    nc.scalar.activation(out=both, in_=both, func=ACT.Sin, scale=-1.0, bias=math.pi / 2)
+
+        for b in range(r_passes):
+            mood(0, b)
+
+        w1_w = [[held("w1_w%d%d" % (b, a), [P, PASS], U32) for a in range(k_passes)] for b in range(r_passes)]
+        w1_s = [[held("w1_s%d%d" % (b, a), [P, PASS], U8) for a in range(k_passes)] for b in range(r_passes)]
+        w3_w = [held("w3_w%d" % b, [P, N], U32) for b in range(r_passes)]
+        w3_s = [held("w3_s%d" % b, [P, N], U8) for b in range(r_passes)]
+        w1_engines = ["gpsimd","scalar","gpsimd","vector"]
+        w3_engines = ["gpsimd","gpsimd"]
+        for b in range(r_passes):
+            for a in range(k_passes):
+                rounded = work.tile([P, PACK * PASS], BF16, name="rounded", align_bytes=64, bufs=3)
+                walk = "t m j" if w1_engines[2 * b + a] == "gpsimd" else "m j t"
+                round_to_bf16(
+                    w1_engines[2 * b + a],
+                    rounded[:].rearrange("p (t m j) -> p " + walk, t=PACK, j=PACK),
+                    w1_raw[b][a][:].rearrange("p j (m t) -> p " + walk, t=PACK),
+                )
+                nc.vector.quantize_mx(out=w1_w[b][a][:].bitcast(FP8X4), scales=w1_s[b][a][:], in_=rounded[:])
+        neg_gain = held("neg_gain", [P, r_passes, PACK], F32)
+        nc.vector.tensor_scalar(out=neg_gain[:], in0=gain_t[:], scalar1=-1.0, scalar2=None, op0=ALU.mult)
+
+        def quantise_w3():
+            for b in range(r_passes):
+                rounded = work.tile([P, PACK * N], BF16, name="rounded", align_bytes=64, bufs=3)
+                walk = "c i j" if w3_engines[b] == "gpsimd" else "c j i"
+                round_to_bf16(
+                    w3_engines[b],
+                    rounded[:].rearrange("p (c i j) -> p " + walk, i=4, j=PACK),
+                    w3_raw[b][:].rearrange("p j (c i) -> p " + walk, i=4),
+                )
+                nc.vector.quantize_mx(out=w3_w[b][:].bitcast(FP8X4), scales=w3_s[b][:], in_=rounded[:])
+
+        def features(c, b):
+            u, first = divmod(c * CHUNK, HALF)
+            half_sine = work.tile([P, PACK, CHUNK], F32, name="slot%d" % b, bufs=1)
+            for pair in range(PACK // 2):
+                bank = psum.tile([P, 2, CHUNK], F32, name="rig_bank")
+                for e in range(2):
+                    t = 2 * pair + e
+                    for a in range(k_passes):
+                        nc.tensor.matmul_mx(
+                            out=bank[:, e, :],
+                            lhsT=w1_w[b][a][:, t * P : (t + 1) * P].bitcast(FP8X4),
+                            lhsT_scale=w1_s[b][a][:, t * P : (t + 1) * P],
+                            rhs=v_w[u][a][:, first : first + CHUNK].bitcast(FP8X4),
+                            rhs_scale=v_s[4 * a : P, c * CHUNK : (c + 1) * CHUNK],
+                            start=(a == 0),
+                            stop=(a == k_passes - 1),
+                        )
+                nc.scalar.activation(
+                    out=half_sine[:, 2 * pair : 2 * pair + 2, :], in_=bank[:], func=ACT.Sin, scale=0.5, bias=-math.pi / 4
+                )
+            versine = half_sine
+            nc.scalar.activation(out=versine[:], in_=half_sine[:], func=ACT.Square, scale=math.sqrt(2.0))
+            gained = work.tile([P, PACK, CHUNK], F32, name="gained", bufs=3)
+            for t in range(PACK):
+                if t < [0,0,4,4,4,4,4,4][2 * c + b]:
+                    nc.scalar.activation(
+                        out=gained[:, t, :], in_=versine[:, t, :], func=ACT.Identity,
+                        scale=neg_gain[:, b, t : t + 1], bias=gain_t[:, b, t : t + 1],
+                    )
+                else:
+                    nc.vector.tensor_scalar(
+                        out=gained[:, t, :], in0=versine[:, t, :], scalar1=neg_gain[:, b, t : t + 1],
+                        scalar2=gain_t[:, b, t : t + 1], op0=ALU.mult, op1=ALU.add,
+                    )
+            h = work.tile([P, PACK * CHUNK], BF16, name="h", align_bytes=64)
+            nc.vector.tensor_tensor(
+                out=h[:].rearrange("p (c i t) -> p c t i", i=4, t=PACK),
+                in0=gained[:].rearrange("p t (c i) -> p c t i", i=4),
+                in1=cos_mood[u][b][:, :, first : first + CHUNK].rearrange("p t (c i) -> p c t i", i=4),
+                op=ALU.mult,
+            )
+            h_w = work.tile([P, CHUNK], U32, name="h_w", align_bytes=64, bufs=4)
+            h_s = work.tile([P, CHUNK], U8, name="h_s", align_bytes=64, bufs=4)
+            nc.vector.quantize_mx(out=h_w[:].bitcast(FP8X4), scales=h_s[:], in_=h[:])
+            return h_w, h_s
+
+        def views(c, pair, hq):
+            bank_a = psum.tile([P, 2, CHUNK], F32, name="ya_bank")
+            bank_b = psum.tile([P, 2, CHUNK], F32, name="yb_bank")
+            for e in range(2):
+                n = 2 * pair + e
+                for b in range(r_passes):
+                    nc.tensor.matmul_mx(
+                        out=bank_b[:, e, :],
+                        lhsT=w4_w[:, b, n * P : (n + 1) * P].bitcast(FP8X4),
+                        lhsT_scale=w4_s[:, b * N + n * P : b * N + (n + 1) * P],
+                        rhs=hq[b][0][:].bitcast(FP8X4),
+                        rhs_scale=hq[b][1][:],
+                        start=(b == 0),
+                        stop=(b == r_passes - 1),
+                    )
+            for e in range(2):
+                n = 2 * pair + e
+                for b in range(r_passes):
+                    nc.tensor.matmul_mx(
+                        out=bank_a[:, e, :],
+                        lhsT=w3_w[b][:, n * P : (n + 1) * P].bitcast(FP8X4),
+                        lhsT_scale=w3_s[b][:, n * P : (n + 1) * P],
+                        rhs=hq[b][0][:].bitcast(FP8X4),
+                        rhs_scale=hq[b][1][:],
+                        start=(b == 0),
+                        stop=(b == r_passes - 1),
+                    )
+            biased = work.tile([P, 2, CHUNK], F32, name="slot%d" % pair, bufs=1)
+            for e in range(2):
+                n = 2 * pair + e
+                nc.scalar.activation(out=biased[:, e, :], in_=bank_b[:, e, :], func=ACT.Identity, bias=b4_t[:, n : n + 1])
+            y = work.tile([P, 2, CHUNK], F32, name="y", bufs=4)
+            nc.vector.tensor_tensor(out=y[:], in0=bank_a[:], in1=biased[:], op=ALU.max)
+            for e in range(2):
+                n = 2 * pair + e
+                nc.vector.tensor_tensor(
+                    pages[n][:].indirect(offs3_t[:, list_cols(c * CHUNK, CHUNK)]),
+                    y[:, e, :],
+                    wgo_t[:, c * CHUNK : (c + 1) * CHUNK],
+                    ALU.mult,
+                )
+                if c == chunks - 1:
+                    nc.sync.dma_start(out[n * P : (n + 1) * P, :], pages[n][:])
+
+        nc.vector.tensor_copy(v2_w[1][:], tab2_w[:].indirect(offs2_t[:, list_cols(HALF, HALF)]))
+        for a in range(k_passes):
+            nc.vector.tensor_copy(v_w[1][a][:], tab_w[a][:].indirect(offs_t[:, list_cols(HALF, HALF)]))
+        hq = [[None] * r_passes for c in range(chunks)]
+        for c in range(chunks + 1):
+            for b in range(r_passes):
+                if c < chunks:
+                    hq[c][b] = features(c, b)
+                if c == 0 and b == r_passes - 1:
+                    quantise_w3()
+                if c > 0:
+                    views(c - 1, b, hq[c - 1])
+                if c == 1:
+                    mood(1, b)

@@ -76,40 +76,47 @@ def tile_list_cue_look_proposer_kernel(
         for plane in (tab_s, w4_s):
             nc.vector.memset(plane[:].bitcast(I32), 0)
 
-        def load_quadrant(plane, rows, q):
-            nc.sync.dma_start(
+        def load_quadrant(queue, plane, rows, q):
+            queue.dma_start(
                 plane[32 * q : 32 * (q + 1), :].bitcast(I32),
                 rows[4 * q : 4 * q + 4, :].bitcast(I32).partition_broadcast(8),
             )
 
+        def load_w1(b, a):
+            nc.sync.dma_start(
+                w1_raw[b][a][:],
+                w1[a * PASS : (a + 1) * PASS, b * PASS : (b + 1) * PASS].rearrange("(p j) c -> p j c", j=PACK),
+            )
+
+        def chunk_of(list_tile, c):
+            return list_tile[:, c * CHUNK // LIST_ROWS : (c + 1) * CHUNK // LIST_ROWS]
+
         nc.sync.dma_start(offs2_t[:], offs2)
         for q in range(4):
-            load_quadrant(tab2_s, tab2_scales[0], q)
+            load_quadrant(nc.sync, tab2_s, tab2_scales[0], q)
         nc.sync.dma_start(tab2_w[:].bitcast(I32), words_view(tab2_words[0]))
         nc.sync.dma_start(w2_raw[:].bitcast(I32), w2_words[0].bitcast(I32))
-        for q in range(4):
-            load_quadrant(w2_raw_s, w2_scales[0], q)
         nc.sync.dma_start(offs_t[:], offs)
-        nc.sync.dma_start(tab_w[0][:].bitcast(I32), words_view(tab_words[0]))
+        for q in range(4):
+            load_quadrant(nc.gpsimd, w2_raw_s, w2_scales[0], q)
         for a in range(k_passes):
             for r in range(2):
                 nc.sync.dma_start(tab_s[4 * a + r : P : 16, :].bitcast(I32), tab_scales[a, r:16:2, :].bitcast(I32))
+        for a in range(k_passes):
+            nc.sync.dma_start(tab_w[a][:].bitcast(I32), words_view(tab_words[a]))
+        for a in range(k_passes):
+            load_w1(0, a)
         nc.sync.dma_start(gain_t[:], gain.rearrange("(b p t) -> p b t", p=P, t=PACK))
-        nc.sync.dma_start(tab_w[1][:].bitcast(I32), words_view(tab_words[1]))
-        for b in range(r_passes):
-            for a in range(k_passes):
-                nc.sync.dma_start(
-                    w1_raw[b][a][:],
-                    w1[a * PASS : (a + 1) * PASS, b * PASS : (b + 1) * PASS].rearrange("(p j) c -> p j c", j=PACK),
-                )
+        for a in range(k_passes):
+            load_w1(1, a)
         for b in range(r_passes):
             nc.sync.dma_start(w3_raw[b][:], w3[b * PASS : (b + 1) * PASS, :].rearrange("(p j) c -> p j c", j=PACK))
+            for q in range(2 * b, 2 * b + 2):
+                nc.sync.dma_start(
+                    w4_s[32 * q : 32 * q + 4, :].bitcast(I32).rearrange("p (a c) -> p a c", a=r_passes),
+                    w4_scales[:, 4 * q : 4 * q + 4, :].bitcast(I32).rearrange("a q c -> q a c"),
+                )
         nc.sync.dma_start(w4_w[:].bitcast(I32), w4_words.rearrange("a p c i -> p a (c i)").bitcast(I32))
-        for q in range(4):
-            nc.sync.dma_start(
-                w4_s[32 * q : 32 * q + 4, :].bitcast(I32).rearrange("p (a c) -> p a c", a=r_passes),
-                w4_scales[:, 4 * q : 4 * q + 4, :].bitcast(I32).rearrange("a q c -> q a c"),
-            )
         with nc.allow_non_contiguous_dma(reason="one bias value a partition"):
             nc.sync.dma_start(b4_t[:], b4.rearrange("(n p) -> p n", p=P))
         nc.sync.dma_start(offs3_t[:], offs3)
@@ -117,15 +124,35 @@ def tile_list_cue_look_proposer_kernel(
         for n in range(n_tiles):
             nc.sync.dma_start(pages[n][:], page1[n * P : (n + 1) * P, :])
 
-        def list_cols(first, count):
-            return slice(first // LIST_ROWS, (first + count) // LIST_ROWS)
+        moods = {}
+        rigs = {}
+        cosines = {}
+        hq = {}
+
+        def look_up_moods(c):
+            name = "v2_w%d" % c if c < 2 else "w1_raw1%d" % (c - 2)
+            moods[c] = held(name, [P, CHUNK], U32)
+            nc.vector.tensor_copy(moods[c][:], tab2_w[:].indirect(chunk_of(offs2_t, c)))
+
+        def look_up_rigs(c):
+            rigs[c] = []
+            for a in range(k_passes):
+                words = work.tile([P, CHUNK], U32, name="v_w%d" % a, align_bytes=64, bufs=2)
+                nc.vector.tensor_copy(words[:], tab_w[a][:].indirect(chunk_of(offs_t, c)))
+                rigs[c].append(words)
 
         v2_s = held("v2_s", [P, S], U8)
-        v2_w = [held("v2_w%d" % u, [P, HALF], U32) for u in range(halves)]
+        nc.vector.tensor_copy(v2_s[:], tab2_s[:].indirect(offs2_t[:]))
+        look_up_moods(0)
+        v_gs = held("v_gs", [P, S], U8)
+        v_s = held("v_s", [P, S], U8)
+        nc.vector.tensor_copy(v_gs[:], tab_s[:].indirect(offs_t[:]))
+        nc.vector.tensor_copy(out=v_s[:].bitcast(I32), in_=v_gs[:].bitcast(I32))
+        for a in range(k_passes):
+            for r in range(2):
+                nc.gpsimd.dma_start(v_s[4 * a + 2 + r : P : 32, :].bitcast(I32), v_gs[16 + 4 * a + r : P : 32, :].bitcast(I32))
         w2_w = held("w2_w", [P, 2 * H], U8)
         w2_s = held("w2_s", [P, H], U8)
-        nc.vector.tensor_copy(v2_s[:], tab2_s[:].indirect(offs2_t[:]))
-        nc.vector.tensor_copy(v2_w[0][:], tab2_w[:].indirect(offs2_t[:, list_cols(0, HALF)]))
         nc.vector.tensor_copy(
             out=w2_w[:].bitcast(U16).rearrange("p (b t m) -> p b m t", b=r_passes, t=PACK),
             in_=w2_raw[:].bitcast(U16).rearrange("p (b m t) -> p b m t", b=r_passes, t=PACK),
@@ -134,75 +161,58 @@ def tile_list_cue_look_proposer_kernel(
             out=w2_s[:].rearrange("p (b t m) -> p b m t", b=r_passes, t=PACK),
             in_=w2_raw_s[:].rearrange("p (b m t) -> p b m t", b=r_passes, t=PACK),
         )
+        look_up_rigs(0)
 
-        v_gs = held("v_gs", [P, S], U8)
-        v_s = held("v_s", [P, S], U8)
-        v_w = [[held("v_w%d%d" % (u, a), [P, HALF], U32) for a in range(k_passes)] for u in range(halves)]
-        nc.vector.tensor_copy(v_gs[:], tab_s[:].indirect(offs_t[:]))
-        nc.vector.tensor_copy(out=v_s[:].bitcast(I32), in_=v_gs[:].bitcast(I32))
-        for a in range(k_passes):
-            for r in range(2):
-                nc.gpsimd.dma_start(v_s[4 * a + 2 + r : P : 32, :].bitcast(I32), v_gs[16 + 4 * a + r : P : 32, :].bitcast(I32))
-        for a in range(k_passes):
-            nc.vector.tensor_copy(v_w[0][a][:], tab_w[a][:].indirect(offs_t[:, list_cols(0, HALF)]))
-
-        cos_mood = [[held("cos%d%d" % (u, b), [P, PACK, HALF], F32) for b in range(r_passes)] for u in range(halves)]
-
-        def mood(u, b):
-            size = cos_mood[u][b]
-            for t in range(PACK):
-                col = b * PASS + t * P
-                bank = psum.tile([P, HALF], F32, name="mood_bank")
-                nc.tensor.matmul_mx(
-                    out=bank[:],
-                    lhsT=w2_w[:, 2 * col : 2 * (col + P)].bitcast(FP4X4),
-                    lhsT_scale=w2_s[:, col : col + P],
-                    rhs=v2_w[u][:].bitcast(FP8X4),
-                    rhs_scale=v2_s[:, u * HALF : (u + 1) * HALF],
-                    start=True,
-                    stop=True,
-                )
-                nc.scalar.activation(out=size[:, t, :], in_=bank[:], func=ACT.Abs)
-                if t % 2 == 1:
-                    both = size[:, t - 1 : t + 1, :]
-                    nc.scalar.activation(out=both, in_=both, func=ACT.Sin, scale=-1.0, bias=math.pi / 2)
-
-        for b in range(r_passes):
-            mood(0, b)
+        def cosine(c, b):
+            cos = work.tile([P, PACK, CHUNK], F32, name="cos", bufs=4)
+            for pair in range(PACK // 2):
+                bank = psum.tile([P, 2, CHUNK], F32, name="mood_bank")
+                for e in range(2):
+                    col = b * PASS + (2 * pair + e) * P
+                    nc.tensor.matmul_mx(
+                        out=bank[:, e, :],
+                        lhsT=w2_w[:, 2 * col : 2 * (col + P)].bitcast(FP4X4),
+                        lhsT_scale=w2_s[:, col : col + P],
+                        rhs=moods[c][:].bitcast(FP8X4),
+                        rhs_scale=v2_s[:, c * CHUNK : (c + 1) * CHUNK],
+                        start=True,
+                        stop=True,
+                    )
+                nc.scalar.activation(out=cos[:, 2 * pair : 2 * pair + 2, :], in_=bank[:], func=ACT.Abs)
+            nc.scalar.activation(out=cos[:], in_=cos[:], func=ACT.Sin, scale=-1.0, bias=math.pi / 2)
+            cosines[c, b] = cos
 
         w1_w = [[held("w1_w%d%d" % (b, a), [P, PASS], U32) for a in range(k_passes)] for b in range(r_passes)]
         w1_s = [[held("w1_s%d%d" % (b, a), [P, PASS], U8) for a in range(k_passes)] for b in range(r_passes)]
         w3_w = [held("w3_w%d" % b, [P, N], U32) for b in range(r_passes)]
         w3_s = [held("w3_s%d" % b, [P, N], U8) for b in range(r_passes)]
-        w1_engines = ["gpsimd","scalar","gpsimd","vector"]
-        w3_engines = ["gpsimd","gpsimd"]
-        for b in range(r_passes):
+        w1_engines = ["vector","vector","vector","vector"]
+        w3_engines = ["vector","vector"]
+
+        def quantise_w1(b):
             for a in range(k_passes):
                 rounded = work.tile([P, PACK * PASS], BF16, name="rounded", align_bytes=64, bufs=3)
-                walk = "t m j" if w1_engines[2 * b + a] == "gpsimd" else "m j t"
                 round_to_bf16(
                     w1_engines[2 * b + a],
-                    rounded[:].rearrange("p (t m j) -> p " + walk, t=PACK, j=PACK),
-                    w1_raw[b][a][:].rearrange("p j (m t) -> p " + walk, t=PACK),
+                    rounded[:].rearrange("p (t m j) -> p m j t", t=PACK, j=PACK),
+                    w1_raw[b][a][:].rearrange("p j (m t) -> p m j t", t=PACK),
                 )
                 nc.vector.quantize_mx(out=w1_w[b][a][:].bitcast(FP8X4), scales=w1_s[b][a][:], in_=rounded[:])
-        neg_gain = held("neg_gain", [P, r_passes, PACK], F32)
-        nc.vector.tensor_scalar(out=neg_gain[:], in0=gain_t[:], scalar1=-1.0, scalar2=None, op0=ALU.mult)
 
         def quantise_w3():
             for b in range(r_passes):
                 rounded = work.tile([P, PACK * N], BF16, name="rounded", align_bytes=64, bufs=3)
-                walk = "c i j" if w3_engines[b] == "gpsimd" else "c j i"
                 round_to_bf16(
                     w3_engines[b],
-                    rounded[:].rearrange("p (c i j) -> p " + walk, i=4, j=PACK),
-                    w3_raw[b][:].rearrange("p j (c i) -> p " + walk, i=4),
+                    rounded[:].rearrange("p (c i j) -> p c j i", i=4, j=PACK),
+                    w3_raw[b][:].rearrange("p j (c i) -> p c j i", i=4),
                 )
                 nc.vector.quantize_mx(out=w3_w[b][:].bitcast(FP8X4), scales=w3_s[b][:], in_=rounded[:])
 
-        def features(c, b):
-            u, first = divmod(c * CHUNK, HALF)
-            half_sine = work.tile([P, PACK, CHUNK], F32, name="slot%d" % b, bufs=1)
+        neg_gain = held("neg_gain", [P, r_passes, PACK], F32)
+
+        def features(step, c, b):
+            sine = work.tile([P, PACK, CHUNK], F32, name="slot%d" % (step % 2), bufs=1)
             for pair in range(PACK // 2):
                 bank = psum.tile([P, 2, CHUNK], F32, name="rig_bank")
                 for e in range(2):
@@ -212,41 +222,40 @@ def tile_list_cue_look_proposer_kernel(
                             out=bank[:, e, :],
                             lhsT=w1_w[b][a][:, t * P : (t + 1) * P].bitcast(FP8X4),
                             lhsT_scale=w1_s[b][a][:, t * P : (t + 1) * P],
-                            rhs=v_w[u][a][:, first : first + CHUNK].bitcast(FP8X4),
+                            rhs=rigs[c][a][:].bitcast(FP8X4),
                             rhs_scale=v_s[4 * a : P, c * CHUNK : (c + 1) * CHUNK],
                             start=(a == 0),
                             stop=(a == k_passes - 1),
                         )
                 nc.scalar.activation(
-                    out=half_sine[:, 2 * pair : 2 * pair + 2, :], in_=bank[:], func=ACT.Sin, scale=0.5, bias=-math.pi / 4
+                    out=sine[:, 2 * pair : 2 * pair + 2, :], in_=bank[:], func=ACT.Sin, scale=0.5, bias=-math.pi / 4
                 )
-            versine = half_sine
-            nc.scalar.activation(out=versine[:], in_=half_sine[:], func=ACT.Square, scale=math.sqrt(2.0))
-            gained = work.tile([P, PACK, CHUNK], F32, name="gained", bufs=3)
+            nc.scalar.activation(out=sine[:], in_=sine[:], func=ACT.Square, scale=math.sqrt(2.0))
+            gained = work.tile([P, PACK, CHUNK], F32, name="gained", bufs=2)
             for t in range(PACK):
-                if t < [0,0,4,4,4,4,4,4][2 * c + b]:
+                if t < [4,4,4,4,4,4,4,4][step]:
                     nc.scalar.activation(
-                        out=gained[:, t, :], in_=versine[:, t, :], func=ACT.Identity,
+                        out=gained[:, t, :], in_=sine[:, t, :], func=ACT.Identity,
                         scale=neg_gain[:, b, t : t + 1], bias=gain_t[:, b, t : t + 1],
                     )
                 else:
                     nc.vector.tensor_scalar(
-                        out=gained[:, t, :], in0=versine[:, t, :], scalar1=neg_gain[:, b, t : t + 1],
+                        out=gained[:, t, :], in0=sine[:, t, :], scalar1=neg_gain[:, b, t : t + 1],
                         scalar2=gain_t[:, b, t : t + 1], op0=ALU.mult, op1=ALU.add,
                     )
             h = work.tile([P, PACK * CHUNK], BF16, name="h", align_bytes=64)
             nc.vector.tensor_tensor(
                 out=h[:].rearrange("p (c i t) -> p c t i", i=4, t=PACK),
                 in0=gained[:].rearrange("p t (c i) -> p c t i", i=4),
-                in1=cos_mood[u][b][:, :, first : first + CHUNK].rearrange("p t (c i) -> p c t i", i=4),
+                in1=cosines[c, b][:].rearrange("p t (c i) -> p c t i", i=4),
                 op=ALU.mult,
             )
-            h_w = work.tile([P, CHUNK], U32, name="h_w", align_bytes=64, bufs=4)
-            h_s = work.tile([P, CHUNK], U8, name="h_s", align_bytes=64, bufs=4)
+            h_w = work.tile([P, CHUNK], U32, name="h_w", align_bytes=64, bufs=6)
+            h_s = work.tile([P, CHUNK], U8, name="h_s", align_bytes=64, bufs=6)
             nc.vector.quantize_mx(out=h_w[:].bitcast(FP8X4), scales=h_s[:], in_=h[:])
-            return h_w, h_s
+            hq[c, b] = (h_w, h_s)
 
-        def views(c, pair, hq):
+        def views(step, c, pair):
             bank_a = psum.tile([P, 2, CHUNK], F32, name="ya_bank")
             bank_b = psum.tile([P, 2, CHUNK], F32, name="yb_bank")
             for e in range(2):
@@ -256,8 +265,8 @@ def tile_list_cue_look_proposer_kernel(
                         out=bank_b[:, e, :],
                         lhsT=w4_w[:, b, n * P : (n + 1) * P].bitcast(FP8X4),
                         lhsT_scale=w4_s[:, b * N + n * P : b * N + (n + 1) * P],
-                        rhs=hq[b][0][:].bitcast(FP8X4),
-                        rhs_scale=hq[b][1][:],
+                        rhs=hq[c, b][0][:].bitcast(FP8X4),
+                        rhs_scale=hq[c, b][1][:],
                         start=(b == 0),
                         stop=(b == r_passes - 1),
                     )
@@ -268,39 +277,46 @@ def tile_list_cue_look_proposer_kernel(
                         out=bank_a[:, e, :],
                         lhsT=w3_w[b][:, n * P : (n + 1) * P].bitcast(FP8X4),
                         lhsT_scale=w3_s[b][:, n * P : (n + 1) * P],
-                        rhs=hq[b][0][:].bitcast(FP8X4),
-                        rhs_scale=hq[b][1][:],
+                        rhs=hq[c, b][0][:].bitcast(FP8X4),
+                        rhs_scale=hq[c, b][1][:],
                         start=(b == 0),
                         stop=(b == r_passes - 1),
                     )
-            biased = work.tile([P, 2, CHUNK], F32, name="slot%d" % pair, bufs=1)
+            biased = work.tile([P, 2, CHUNK], F32, name="slot%d" % (step % 2), bufs=1)
             for e in range(2):
                 n = 2 * pair + e
                 nc.scalar.activation(out=biased[:, e, :], in_=bank_b[:, e, :], func=ACT.Identity, bias=b4_t[:, n : n + 1])
-            y = work.tile([P, 2, CHUNK], F32, name="y", bufs=4)
+            y = work.tile([P, 2, CHUNK], F32, name="y", bufs=2)
             nc.vector.tensor_tensor(out=y[:], in0=bank_a[:], in1=biased[:], op=ALU.max)
             for e in range(2):
                 n = 2 * pair + e
                 nc.vector.tensor_tensor(
-                    pages[n][:].indirect(offs3_t[:, list_cols(c * CHUNK, CHUNK)]),
-                    y[:, e, :],
-                    wgo_t[:, c * CHUNK : (c + 1) * CHUNK],
-                    ALU.mult,
+                    pages[n][:].indirect(chunk_of(offs3_t, c)), y[:, e, :], wgo_t[:, c * CHUNK : (c + 1) * CHUNK], ALU.mult
                 )
                 if c == chunks - 1:
                     nc.sync.dma_start(out[n * P : (n + 1) * P, :], pages[n][:])
 
-        nc.vector.tensor_copy(v2_w[1][:], tab2_w[:].indirect(offs2_t[:, list_cols(HALF, HALF)]))
-        for a in range(k_passes):
-            nc.vector.tensor_copy(v_w[1][a][:], tab_w[a][:].indirect(offs_t[:, list_cols(HALF, HALF)]))
-        hq = [[None] * r_passes for c in range(chunks)]
-        for c in range(chunks + 1):
-            for b in range(r_passes):
-                if c < chunks:
-                    hq[c][b] = features(c, b)
-                if c == 0 and b == r_passes - 1:
-                    quantise_w3()
-                if c > 0:
-                    views(c - 1, b, hq[c - 1])
-                if c == 1:
-                    mood(1, b)
+        steps = [(0, 0), (1, 0), (0, 1), (1, 1)] + [(c, b) for c in range(2, chunks) for b in range(r_passes)]
+        cosine(0, 0)
+        quantise_w1(0)
+        nc.vector.tensor_scalar(out=neg_gain[:], in0=gain_t[:], scalar1=-1.0, scalar2=None, op0=ALU.mult)
+        quantise_w1(1)
+        for c in range(1, chunks):
+            look_up_moods(c)
+        look_up_rigs(1)
+        for c, b in steps[1:1]:
+            cosine(c, b)
+        last = len(steps) - 1
+        for step in range(len(steps) + 2):
+            if step + 1 <= last:
+                cosine(*steps[step + 1])
+
+            if step <= last:
+                c, b = steps[step]
+                features(step, c, b)
+                if b == 1 and c + 2 < chunks:
+                    look_up_rigs(c + 2)
+            if step == 1:
+                quantise_w3()
+            if step >= 2:
+                views(step, *divmod(step - 2, 2))

@@ -94,35 +94,29 @@ def tile_list_cue_look_proposer_kernel(
         nc.sync.dma_start(offs2_t[:], offs2)
         for q in range(4):
             load_quadrant(nc.sync, tab2_s, tab2_scales[0], q)
-        nc.sync.dma_start(tab2_w[:].bitcast(I32), words_view(tab2_words[0]))
         nc.sync.dma_start(w2_raw[:].bitcast(I32), w2_words[0].bitcast(I32))
+        nc.sync.dma_start(tab2_w[:].bitcast(I32), words_view(tab2_words[0]))
         nc.sync.dma_start(offs_t[:], offs)
         for q in range(4):
-            load_quadrant(nc.gpsimd, w2_raw_s, w2_scales[0], q)
+            load_quadrant(nc.sync, w2_raw_s, w2_scales[0], q)
+        nc.sync.dma_start(tab_w[0][:].bitcast(I32), words_view(tab_words[0]))
         for a in range(k_passes):
             for r in range(2):
                 nc.sync.dma_start(tab_s[4 * a + r : P : 16, :].bitcast(I32), tab_scales[a, r:16:2, :].bitcast(I32))
-        for a in range(k_passes):
-            nc.sync.dma_start(tab_w[a][:].bitcast(I32), words_view(tab_words[a]))
-        for a in range(k_passes):
-            load_w1(0, a)
+        nc.sync.dma_start(tab_w[1][:].bitcast(I32), words_view(tab_words[1]))
         nc.sync.dma_start(gain_t[:], gain.rearrange("(b p t) -> p b t", p=P, t=PACK))
-        for a in range(k_passes):
-            load_w1(1, a)
-        for b in range(r_passes):
-            nc.sync.dma_start(w3_raw[b][:], w3[b * PASS : (b + 1) * PASS, :].rearrange("(p j) c -> p j c", j=PACK))
-            for q in range(2 * b, 2 * b + 2):
-                nc.sync.dma_start(
-                    w4_s[32 * q : 32 * q + 4, :].bitcast(I32).rearrange("p (a c) -> p a c", a=r_passes),
-                    w4_scales[:, 4 * q : 4 * q + 4, :].bitcast(I32).rearrange("a q c -> q a c"),
-                )
-        nc.sync.dma_start(w4_w[:].bitcast(I32), w4_words.rearrange("a p c i -> p a (c i)").bitcast(I32))
+        nc.sync.dma_start(offs3_t[:], offs3)
+        load_w1(0, 0)
+        load_w1(0, 1)
+        load_w1(1, 0)
         with nc.allow_non_contiguous_dma(reason="one bias value a partition"):
             nc.sync.dma_start(b4_t[:], b4.rearrange("(n p) -> p n", p=P))
-        nc.sync.dma_start(offs3_t[:], offs3)
-        nc.sync.dma_start(wgo_t[:], wgo)
-        for n in range(n_tiles):
-            nc.sync.dma_start(pages[n][:], page1[n * P : (n + 1) * P, :])
+        for q in range(0, 1):
+            nc.sync.dma_start(
+                w4_s[32 * q : 32 * q + 4, :].bitcast(I32).rearrange("p (a c) -> p a c", a=r_passes),
+                w4_scales[:, 4 * q : 4 * q + 4, :].bitcast(I32).rearrange("a q c -> q a c"),
+            )
+
 
         moods = {}
         rigs = {}
@@ -130,27 +124,18 @@ def tile_list_cue_look_proposer_kernel(
         hq = {}
 
         def look_up_moods(c):
-            name = "v2_w%d" % c if c < 2 else "w1_raw1%d" % (c - 2)
+            name = ["v2_w", "w2_raw_s", "w1_raw10", "w1_raw11"][c]
             moods[c] = held(name, [P, CHUNK], U32)
             nc.vector.tensor_copy(moods[c][:], tab2_w[:].indirect(chunk_of(offs2_t, c)))
 
         def look_up_rigs(c):
-            rigs[c] = []
+            rigs[c] = held(["v_w", "w1_raw01", "spare2", "spare3"][c], [P, k_passes, CHUNK], U32)
             for a in range(k_passes):
-                words = work.tile([P, CHUNK], U32, name="v_w%d" % a, align_bytes=64, bufs=2)
-                nc.vector.tensor_copy(words[:], tab_w[a][:].indirect(chunk_of(offs_t, c)))
-                rigs[c].append(words)
+                nc.vector.tensor_copy(rigs[c][:, a, :], tab_w[a][:].indirect(chunk_of(offs_t, c)))
 
         v2_s = held("v2_s", [P, S], U8)
         nc.vector.tensor_copy(v2_s[:], tab2_s[:].indirect(offs2_t[:]))
         look_up_moods(0)
-        v_gs = held("v_gs", [P, S], U8)
-        v_s = held("v_s", [P, S], U8)
-        nc.vector.tensor_copy(v_gs[:], tab_s[:].indirect(offs_t[:]))
-        nc.vector.tensor_copy(out=v_s[:].bitcast(I32), in_=v_gs[:].bitcast(I32))
-        for a in range(k_passes):
-            for r in range(2):
-                nc.gpsimd.dma_start(v_s[4 * a + 2 + r : P : 32, :].bitcast(I32), v_gs[16 + 4 * a + r : P : 32, :].bitcast(I32))
         w2_w = held("w2_w", [P, 2 * H], U8)
         w2_s = held("w2_s", [P, H], U8)
         nc.vector.tensor_copy(
@@ -161,6 +146,25 @@ def tile_list_cue_look_proposer_kernel(
             out=w2_s[:].rearrange("p (b t m) -> p b m t", b=r_passes, t=PACK),
             in_=w2_raw_s[:].rearrange("p (b m t) -> p b m t", b=r_passes, t=PACK),
         )
+        v_gs = held("v_gs", [P, S], U8)
+        v_s = held("v_s", [P, S], U8)
+        nc.vector.tensor_copy(v_gs[:], tab_s[:].indirect(offs_t[:]))
+        nc.vector.tensor_copy(out=v_s[:].bitcast(I32), in_=v_gs[:].bitcast(I32))
+        for a in range(k_passes):
+            for r in range(2):
+                nc.sync.dma_start(v_s[4 * a + 2 + r : P : 32, :].bitcast(I32), v_gs[16 + 4 * a + r : P : 32, :].bitcast(I32))
+        load_w1(1, 1)
+        for b in range(r_passes):
+            nc.sync.dma_start(w3_raw[b][:], w3[b * PASS : (b + 1) * PASS, :].rearrange("(p j) c -> p j c", j=PACK))
+        for q in range(1, 4):
+            nc.sync.dma_start(
+                w4_s[32 * q : 32 * q + 4, :].bitcast(I32).rearrange("p (a c) -> p a c", a=r_passes),
+                w4_scales[:, 4 * q : 4 * q + 4, :].bitcast(I32).rearrange("a q c -> q a c"),
+            )
+        nc.sync.dma_start(w4_w[:].bitcast(I32), w4_words.rearrange("a p c i -> p a (c i)").bitcast(I32))
+        nc.sync.dma_start(wgo_t[:], wgo)
+        for n in range(n_tiles):
+            nc.sync.dma_start(pages[n][:], page1[n * P : (n + 1) * P, :])
         look_up_rigs(0)
 
         def cosine(c, b):
@@ -222,7 +226,7 @@ def tile_list_cue_look_proposer_kernel(
                             out=bank[:, e, :],
                             lhsT=w1_w[b][a][:, t * P : (t + 1) * P].bitcast(FP8X4),
                             lhsT_scale=w1_s[b][a][:, t * P : (t + 1) * P],
-                            rhs=rigs[c][a][:].bitcast(FP8X4),
+                            rhs=rigs[c][:, a, :].bitcast(FP8X4),
                             rhs_scale=v_s[4 * a : P, c * CHUNK : (c + 1) * CHUNK],
                             start=(a == 0),
                             stop=(a == k_passes - 1),
@@ -231,7 +235,10 @@ def tile_list_cue_look_proposer_kernel(
                     out=sine[:, 2 * pair : 2 * pair + 2, :], in_=bank[:], func=ACT.Sin, scale=0.5, bias=-math.pi / 4
                 )
             nc.scalar.activation(out=sine[:], in_=sine[:], func=ACT.Square, scale=math.sqrt(2.0))
-            gained = work.tile([P, PACK, CHUNK], F32, name="gained", bufs=2)
+            if step in (2, 3):
+                gained = held("spare%d" % step, [P, PACK, CHUNK], F32)
+            else:
+                gained = work.tile([P, PACK, CHUNK], F32, name="gained", bufs=2)
             for t in range(PACK):
                 if t < [4,4,4,4,4,4,4,4][step]:
                     nc.scalar.activation(

@@ -109,9 +109,7 @@ def tile_list_cue_look_proposer_kernel(
         load_w1(0, 0)
         load_w1(0, 1)
         load_w1(1, 0)
-        with nc.allow_non_contiguous_dma(reason="one bias value a partition"):
-            nc.sync.dma_start(b4_t[:], b4.rearrange("(n p) -> p n", p=P))
-        for q in range(0, 1):
+        for q in range(0, 2):
             nc.sync.dma_start(
                 w4_s[32 * q : 32 * q + 4, :].bitcast(I32).rearrange("p (a c) -> p a c", a=r_passes),
                 w4_scales[:, 4 * q : 4 * q + 4, :].bitcast(I32).rearrange("a q c -> q a c"),
@@ -156,13 +154,15 @@ def tile_list_cue_look_proposer_kernel(
         load_w1(1, 1)
         for b in range(r_passes):
             nc.sync.dma_start(w3_raw[b][:], w3[b * PASS : (b + 1) * PASS, :].rearrange("(p j) c -> p j c", j=PACK))
-        for q in range(1, 4):
+        for q in range(2, 4):
             nc.sync.dma_start(
                 w4_s[32 * q : 32 * q + 4, :].bitcast(I32).rearrange("p (a c) -> p a c", a=r_passes),
                 w4_scales[:, 4 * q : 4 * q + 4, :].bitcast(I32).rearrange("a q c -> q a c"),
             )
         nc.sync.dma_start(w4_w[:].bitcast(I32), w4_words.rearrange("a p c i -> p a (c i)").bitcast(I32))
         nc.sync.dma_start(wgo_t[:], wgo)
+        with nc.allow_non_contiguous_dma(reason="one bias value a partition"):
+            nc.sync.dma_start(b4_t[:], b4.rearrange("(n p) -> p n", p=P))
         for n in range(n_tiles):
             nc.sync.dma_start(pages[n][:], page1[n * P : (n + 1) * P, :])
         look_up_rigs(0)
@@ -252,9 +252,9 @@ def tile_list_cue_look_proposer_kernel(
                     )
             h = work.tile([P, PACK * CHUNK], BF16, name="h", align_bytes=64)
             nc.vector.tensor_tensor(
-                out=h[:].rearrange("p (c i t) -> p c t i", i=4, t=PACK),
-                in0=gained[:].rearrange("p t (c i) -> p c t i", i=4),
-                in1=cosines[c, b][:].rearrange("p t (c i) -> p c t i", i=4),
+                out=h[:].rearrange("p (c i t) -> p c t i", i=2, t=PACK),
+                in0=gained[:].rearrange("p t (c i) -> p c t i", i=2),
+                in1=cosines[c, b][:].rearrange("p t (c i) -> p c t i", i=2),
                 op=ALU.mult,
             )
             h_w = work.tile([P, CHUNK], U32, name="h_w", align_bytes=64, bufs=6)

@@ -20,9 +20,11 @@ ALU = mybir.AluOpType
 P = 128
 PACK = 4
 PASS = P * PACK
+GROUP = 16
+QUADRANT = 32
+ROWS = 4
 CHUNK = 256
-HALF = 512
-LIST_ROWS = 16
+LAG = 2
 
 
 def tile_list_cue_look_proposer_kernel(
@@ -34,18 +36,7 @@ def tile_list_cue_look_proposer_kernel(
     r_passes = H // PASS
     n_tiles = N // P
     chunks = S // CHUNK
-    halves = S // HALF
-
-    def words_view(dram_words):
-        return dram_words.rearrange("p t i -> p (t i)").bitcast(I32)
-
-    def round_to_bf16(engine, dst, src):
-        if engine == "vector":
-            nc.vector.tensor_copy(out=dst, in_=src)
-        elif engine == "scalar":
-            nc.scalar.activation(out=dst, in_=src, func=ACT.Copy)
-        else:
-            nc.gpsimd.tensor_scalar(out=dst, in0=src, scalar1=1.0, scalar2=0.0, op0=ALU.mult, op1=ALU.add)
+    quadrants = P // QUADRANT
 
     with ExitStack() as ctx:
         keep = ctx.enter_context(tc.tile_pool(name="keep", bufs=1))
@@ -55,9 +46,9 @@ def tile_list_cue_look_proposer_kernel(
         def held(name, shape, dtype):
             return keep.tile(shape, dtype, name=name, align_bytes=64)
 
-        offs_t = held("offs_t", [P, S // LIST_ROWS], U16)
-        offs2_t = held("offs2_t", [P, S // LIST_ROWS], U16)
-        offs3_t = held("offs3_t", [P, S // LIST_ROWS], U16)
+        offs_t = held("offs_t", [P, S // GROUP], U16)
+        offs2_t = held("offs2_t", [P, S // GROUP], U16)
+        offs3_t = held("offs3_t", [P, S // GROUP], U16)
         tab_w = [held("tab_w%d" % a, [P, T], U32) for a in range(k_passes)]
         tab_s = held("tab_s", [P, T], U8)
         tab2_w = held("tab2_w", [P, T], U32)
@@ -73,14 +64,25 @@ def tile_list_cue_look_proposer_kernel(
         wgo_t = held("wgo_t", [P, S], F32)
         pages = [held("page%d" % n, [P, T2], F32) for n in range(n_tiles)]
 
-        for plane in (tab_s, w4_s):
-            nc.vector.memset(plane[:].bitcast(I32), 0)
+        for scale_tile in (tab_s, w4_s):
+            nc.vector.memset(scale_tile[:].bitcast(I32), 0)
 
-        def load_quadrant(queue, plane, rows, q):
-            queue.dma_start(
-                plane[32 * q : 32 * (q + 1), :].bitcast(I32),
-                rows[4 * q : 4 * q + 4, :].bitcast(I32).partition_broadcast(8),
-            )
+        def load_words(tile, dram_words):
+            nc.sync.dma_start(tile[:].bitcast(I32), dram_words.rearrange("p c i -> p (c i)").bitcast(I32))
+
+        def load_scales_repeated(scale_tile, rows):
+            for d in range(quadrants):
+                nc.sync.dma_start(
+                    scale_tile[QUADRANT * d : QUADRANT * (d + 1), :].bitcast(I32),
+                    rows[ROWS * d : ROWS * (d + 1), :].bitcast(I32).partition_broadcast(QUADRANT // ROWS),
+                )
+
+        def load_w4_scales(some_quadrants):
+            for d in some_quadrants:
+                nc.sync.dma_start(
+                    w4_s[QUADRANT * d : QUADRANT * d + ROWS, :].bitcast(I32).rearrange("p (b c) -> p b c", b=r_passes),
+                    w4_scales[:, ROWS * d : ROWS * (d + 1), :].bitcast(I32).rearrange("b q c -> q b c"),
+                )
 
         def load_w1(b, a):
             nc.sync.dma_start(
@@ -88,51 +90,56 @@ def tile_list_cue_look_proposer_kernel(
                 w1[a * PASS : (a + 1) * PASS, b * PASS : (b + 1) * PASS].rearrange("(p j) c -> p j c", j=PACK),
             )
 
-        def chunk_of(list_tile, c):
-            return list_tile[:, c * CHUNK // LIST_ROWS : (c + 1) * CHUNK // LIST_ROWS]
+        def entries(list_tile, c):
+            return list_tile[:, c * CHUNK // GROUP : (c + 1) * CHUNK // GROUP]
 
         nc.sync.dma_start(offs2_t[:], offs2)
-        for q in range(4):
-            load_quadrant(nc.sync, tab2_s, tab2_scales[0], q)
+        load_scales_repeated(tab2_s, tab2_scales[0])
         nc.sync.dma_start(w2_raw[:].bitcast(I32), w2_words[0].bitcast(I32))
-        nc.sync.dma_start(tab2_w[:].bitcast(I32), words_view(tab2_words[0]))
+        load_words(tab2_w, tab2_words[0])
         nc.sync.dma_start(offs_t[:], offs)
-        for q in range(4):
-            load_quadrant(nc.sync, w2_raw_s, w2_scales[0], q)
-        nc.sync.dma_start(tab_w[0][:].bitcast(I32), words_view(tab_words[0]))
+        load_scales_repeated(w2_raw_s, w2_scales[0])
+        load_words(tab_w[0], tab_words[0])
         for a in range(k_passes):
             for r in range(2):
-                nc.sync.dma_start(tab_s[4 * a + r : P : 16, :].bitcast(I32), tab_scales[a, r:16:2, :].bitcast(I32))
-        nc.sync.dma_start(tab_w[1][:].bitcast(I32), words_view(tab_words[1]))
+                nc.sync.dma_start(tab_s[ROWS * a + r : P : GROUP, :].bitcast(I32), tab_scales[a, r::2, :].bitcast(I32))
+        load_words(tab_w[1], tab_words[1])
         nc.sync.dma_start(gain_t[:], gain.rearrange("(b p t) -> p b t", p=P, t=PACK))
         nc.sync.dma_start(offs3_t[:], offs3)
         load_w1(0, 0)
         load_w1(0, 1)
         load_w1(1, 0)
-        for q in range(0, 2):
-            nc.sync.dma_start(
-                w4_s[32 * q : 32 * q + 4, :].bitcast(I32).rearrange("p (a c) -> p a c", a=r_passes),
-                w4_scales[:, 4 * q : 4 * q + 4, :].bitcast(I32).rearrange("a q c -> q a c"),
-            )
-
+        load_w4_scales(range(quadrants // 2))
 
         moods = {}
         rigs = {}
         cosines = {}
-        hq = {}
+        h_quantised = {}
+
+        mood_buffers = [
+            "mood_words",
+            "w2_raw_s",
+            "rig_words",
+            "w1_raw01",
+        ]
+        rig_buffers = [
+            "rig_words",
+            "w1_raw01",
+            "gained2",
+            "gained3",
+        ]
 
         def look_up_moods(c):
-            name = ["v2_w", "w2_raw_s", "w1_raw10", "w1_raw11"][c]
-            moods[c] = held(name, [P, CHUNK], U32)
-            nc.vector.tensor_copy(moods[c][:], tab2_w[:].indirect(chunk_of(offs2_t, c)))
+            moods[c] = held(mood_buffers[c], [P, CHUNK], U32)
+            nc.vector.tensor_copy(moods[c][:], tab2_w[:].indirect(entries(offs2_t, c)))
 
         def look_up_rigs(c):
-            rigs[c] = held(["v_w", "w1_raw01", "spare2", "spare3"][c], [P, k_passes, CHUNK], U32)
+            rigs[c] = held(rig_buffers[c], [P, k_passes, CHUNK], U32)
             for a in range(k_passes):
-                nc.vector.tensor_copy(rigs[c][:, a, :], tab_w[a][:].indirect(chunk_of(offs_t, c)))
+                nc.vector.tensor_copy(rigs[c][:, a, :], tab_w[a][:].indirect(entries(offs_t, c)))
 
-        v2_s = held("v2_s", [P, S], U8)
-        nc.vector.tensor_copy(v2_s[:], tab2_s[:].indirect(offs2_t[:]))
+        mood_s = held("mood_s", [P, S], U8)
+        nc.vector.tensor_copy(mood_s[:], tab2_s[:].indirect(offs2_t[:]))
         look_up_moods(0)
         w2_w = held("w2_w", [P, 2 * H], U8)
         w2_s = held("w2_s", [P, H], U8)
@@ -144,22 +151,23 @@ def tile_list_cue_look_proposer_kernel(
             out=w2_s[:].rearrange("p (b t m) -> p b m t", b=r_passes, t=PACK),
             in_=w2_raw_s[:].rearrange("p (b m t) -> p b m t", b=r_passes, t=PACK),
         )
-        v_gs = held("v_gs", [P, S], U8)
-        v_s = held("v_s", [P, S], U8)
-        nc.vector.tensor_copy(v_gs[:], tab_s[:].indirect(offs_t[:]))
-        nc.vector.tensor_copy(out=v_s[:].bitcast(I32), in_=v_gs[:].bitcast(I32))
+
+        rig_s_by_list = held("rig_s_by_list", [P, S], U8)
+        rig_s = held("rig_s", [P, S], U8)
+        nc.vector.tensor_copy(rig_s_by_list[:], tab_s[:].indirect(offs_t[:]))
+        nc.vector.tensor_copy(out=rig_s[:].bitcast(I32), in_=rig_s_by_list[:].bitcast(I32))
         for a in range(k_passes):
             for r in range(2):
-                nc.sync.dma_start(v_s[4 * a + 2 + r : P : 32, :].bitcast(I32), v_gs[16 + 4 * a + r : P : 32, :].bitcast(I32))
+                nc.sync.dma_start(
+                    rig_s[ROWS * a + 2 + r : P : QUADRANT, :].bitcast(I32),
+                    rig_s_by_list[GROUP + ROWS * a + r : P : QUADRANT, :].bitcast(I32),
+                )
+
         load_w1(1, 1)
         for b in range(r_passes):
             nc.sync.dma_start(w3_raw[b][:], w3[b * PASS : (b + 1) * PASS, :].rearrange("(p j) c -> p j c", j=PACK))
-        for q in range(2, 4):
-            nc.sync.dma_start(
-                w4_s[32 * q : 32 * q + 4, :].bitcast(I32).rearrange("p (a c) -> p a c", a=r_passes),
-                w4_scales[:, 4 * q : 4 * q + 4, :].bitcast(I32).rearrange("a q c -> q a c"),
-            )
-        nc.sync.dma_start(w4_w[:].bitcast(I32), w4_words.rearrange("a p c i -> p a (c i)").bitcast(I32))
+        load_w4_scales(range(quadrants // 2, quadrants))
+        nc.sync.dma_start(w4_w[:].bitcast(I32), w4_words.rearrange("b p c i -> p b (c i)").bitcast(I32))
         nc.sync.dma_start(wgo_t[:], wgo)
         with nc.allow_non_contiguous_dma(reason="one bias value a partition"):
             nc.sync.dma_start(b4_t[:], b4.rearrange("(n p) -> p n", p=P))
@@ -178,7 +186,7 @@ def tile_list_cue_look_proposer_kernel(
                         lhsT=w2_w[:, 2 * col : 2 * (col + P)].bitcast(FP4X4),
                         lhsT_scale=w2_s[:, col : col + P],
                         rhs=moods[c][:].bitcast(FP8X4),
-                        rhs_scale=v2_s[:, c * CHUNK : (c + 1) * CHUNK],
+                        rhs_scale=mood_s[:, c * CHUNK : (c + 1) * CHUNK],
                         start=True,
                         stop=True,
                     )
@@ -190,33 +198,29 @@ def tile_list_cue_look_proposer_kernel(
         w1_s = [[held("w1_s%d%d" % (b, a), [P, PASS], U8) for a in range(k_passes)] for b in range(r_passes)]
         w3_w = [held("w3_w%d" % b, [P, N], U32) for b in range(r_passes)]
         w3_s = [held("w3_s%d" % b, [P, N], U8) for b in range(r_passes)]
-        w1_engines = ["vector","vector","vector","vector"]
-        w3_engines = ["vector","vector"]
+
+        def round_and_quantise(raw_view, pattern, sizes, words, scale_tile):
+            rounded = work.tile([P, PACK * PASS], BF16, name="rounded", align_bytes=64, bufs=3)
+            nc.vector.tensor_copy(out=rounded[:].rearrange(pattern, **sizes), in_=raw_view)
+            nc.vector.quantize_mx(out=words[:].bitcast(FP8X4), scales=scale_tile[:], in_=rounded[:])
 
         def quantise_w1(b):
             for a in range(k_passes):
-                rounded = work.tile([P, PACK * PASS], BF16, name="rounded", align_bytes=64, bufs=3)
-                round_to_bf16(
-                    w1_engines[2 * b + a],
-                    rounded[:].rearrange("p (t m j) -> p m j t", t=PACK, j=PACK),
-                    w1_raw[b][a][:].rearrange("p j (m t) -> p m j t", t=PACK),
-                )
-                nc.vector.quantize_mx(out=w1_w[b][a][:].bitcast(FP8X4), scales=w1_s[b][a][:], in_=rounded[:])
+                raw_view = w1_raw[b][a][:].rearrange("p j (m t) -> p m j t", t=PACK)
+                round_and_quantise(raw_view, "p (t m j) -> p m j t", dict(t=PACK, j=PACK), w1_w[b][a], w1_s[b][a])
 
         def quantise_w3():
             for b in range(r_passes):
-                rounded = work.tile([P, PACK * N], BF16, name="rounded", align_bytes=64, bufs=3)
-                round_to_bf16(
-                    w3_engines[b],
-                    rounded[:].rearrange("p (c i j) -> p c j i", i=4, j=PACK),
-                    w3_raw[b][:].rearrange("p j (c i) -> p c j i", i=4),
-                )
-                nc.vector.quantize_mx(out=w3_w[b][:].bitcast(FP8X4), scales=w3_s[b][:], in_=rounded[:])
+                raw_view = w3_raw[b][:].rearrange("p j (c i) -> p c j i", i=4)
+                round_and_quantise(raw_view, "p (c i j) -> p c j i", dict(i=4, j=PACK), w3_w[b], w3_s[b])
 
         neg_gain = held("neg_gain", [P, r_passes, PACK], F32)
 
+        def scalar_buffer(step, shape):
+            return work.tile(shape, F32, name="scalar_buffer%d" % (step % 2), bufs=1)
+
         def features(step, c, b):
-            sine = work.tile([P, PACK, CHUNK], F32, name="slot%d" % (step % 2), bufs=1)
+            sine = scalar_buffer(step, [P, PACK, CHUNK])
             for pair in range(PACK // 2):
                 bank = psum.tile([P, 2, CHUNK], F32, name="rig_bank")
                 for e in range(2):
@@ -227,7 +231,7 @@ def tile_list_cue_look_proposer_kernel(
                             lhsT=w1_w[b][a][:, t * P : (t + 1) * P].bitcast(FP8X4),
                             lhsT_scale=w1_s[b][a][:, t * P : (t + 1) * P],
                             rhs=rigs[c][:, a, :].bitcast(FP8X4),
-                            rhs_scale=v_s[4 * a : P, c * CHUNK : (c + 1) * CHUNK],
+                            rhs_scale=rig_s[ROWS * a : P, c * CHUNK : (c + 1) * CHUNK],
                             start=(a == 0),
                             stop=(a == k_passes - 1),
                         )
@@ -235,21 +239,16 @@ def tile_list_cue_look_proposer_kernel(
                     out=sine[:, 2 * pair : 2 * pair + 2, :], in_=bank[:], func=ACT.Sin, scale=0.5, bias=-math.pi / 4
                 )
             nc.scalar.activation(out=sine[:], in_=sine[:], func=ACT.Square, scale=math.sqrt(2.0))
-            if step in (2, 3):
-                gained = held("spare%d" % step, [P, PACK, CHUNK], F32)
+            gained_name = "gained%d" % step
+            if gained_name in rig_buffers:
+                gained = held(gained_name, [P, PACK, CHUNK], F32)
             else:
-                gained = work.tile([P, PACK, CHUNK], F32, name="gained", bufs=2)
+                gained = work.tile([P, PACK, CHUNK], F32, name="gained")
             for t in range(PACK):
-                if t < [4,4,4,4,4,4,4,4][step]:
-                    nc.scalar.activation(
-                        out=gained[:, t, :], in_=sine[:, t, :], func=ACT.Identity,
-                        scale=neg_gain[:, b, t : t + 1], bias=gain_t[:, b, t : t + 1],
-                    )
-                else:
-                    nc.vector.tensor_scalar(
-                        out=gained[:, t, :], in0=sine[:, t, :], scalar1=neg_gain[:, b, t : t + 1],
-                        scalar2=gain_t[:, b, t : t + 1], op0=ALU.mult, op1=ALU.add,
-                    )
+                nc.scalar.activation(
+                    out=gained[:, t, :], in_=sine[:, t, :], func=ACT.Identity,
+                    scale=neg_gain[:, b, t : t + 1], bias=gain_t[:, b, t : t + 1],
+                )
             h = work.tile([P, PACK * CHUNK], BF16, name="h", align_bytes=64)
             nc.vector.tensor_tensor(
                 out=h[:].rearrange("p (c i t) -> p c t i", i=2, t=PACK),
@@ -260,70 +259,70 @@ def tile_list_cue_look_proposer_kernel(
             h_w = work.tile([P, CHUNK], U32, name="h_w", align_bytes=64, bufs=6)
             h_s = work.tile([P, CHUNK], U8, name="h_s", align_bytes=64, bufs=6)
             nc.vector.quantize_mx(out=h_w[:].bitcast(FP8X4), scales=h_s[:], in_=h[:])
-            hq[c, b] = (h_w, h_s)
+            h_quantised[c, b] = (h_w, h_s)
 
-        def views(step, c, pair):
-            bank_a = psum.tile([P, 2, CHUNK], F32, name="ya_bank")
-            bank_b = psum.tile([P, 2, CHUNK], F32, name="yb_bank")
+        def second_product(bank, c, pair, words_of, scales_of):
             for e in range(2):
                 n = 2 * pair + e
                 for b in range(r_passes):
+                    h_w, h_s = h_quantised[c, b]
                     nc.tensor.matmul_mx(
-                        out=bank_b[:, e, :],
-                        lhsT=w4_w[:, b, n * P : (n + 1) * P].bitcast(FP8X4),
-                        lhsT_scale=w4_s[:, b * N + n * P : b * N + (n + 1) * P],
-                        rhs=hq[c, b][0][:].bitcast(FP8X4),
-                        rhs_scale=hq[c, b][1][:],
+                        out=bank[:, e, :],
+                        lhsT=words_of(b, n).bitcast(FP8X4),
+                        lhsT_scale=scales_of(b, n),
+                        rhs=h_w[:].bitcast(FP8X4),
+                        rhs_scale=h_s[:],
                         start=(b == 0),
                         stop=(b == r_passes - 1),
                     )
+
+        def view(step, c, pair):
+            ya_bank = psum.tile([P, 2, CHUNK], F32, name="ya_bank")
+            yb_bank = psum.tile([P, 2, CHUNK], F32, name="yb_bank")
+            second_product(
+                yb_bank, c, pair,
+                lambda b, n: w4_w[:, b, n * P : (n + 1) * P],
+                lambda b, n: w4_s[:, b * N + n * P : b * N + (n + 1) * P],
+            )
+            second_product(
+                ya_bank, c, pair,
+                lambda b, n: w3_w[b][:, n * P : (n + 1) * P],
+                lambda b, n: w3_s[b][:, n * P : (n + 1) * P],
+            )
+            biased = scalar_buffer(step, [P, 2, CHUNK])
             for e in range(2):
                 n = 2 * pair + e
-                for b in range(r_passes):
-                    nc.tensor.matmul_mx(
-                        out=bank_a[:, e, :],
-                        lhsT=w3_w[b][:, n * P : (n + 1) * P].bitcast(FP8X4),
-                        lhsT_scale=w3_s[b][:, n * P : (n + 1) * P],
-                        rhs=hq[c, b][0][:].bitcast(FP8X4),
-                        rhs_scale=hq[c, b][1][:],
-                        start=(b == 0),
-                        stop=(b == r_passes - 1),
-                    )
-            biased = work.tile([P, 2, CHUNK], F32, name="slot%d" % (step % 2), bufs=1)
-            for e in range(2):
-                n = 2 * pair + e
-                nc.scalar.activation(out=biased[:, e, :], in_=bank_b[:, e, :], func=ACT.Identity, bias=b4_t[:, n : n + 1])
-            y = work.tile([P, 2, CHUNK], F32, name="y", bufs=2)
-            nc.vector.tensor_tensor(out=y[:], in0=bank_a[:], in1=biased[:], op=ALU.max)
+                nc.scalar.activation(out=biased[:, e, :], in_=yb_bank[:, e, :], func=ACT.Identity, bias=b4_t[:, n : n + 1])
+            y = work.tile([P, 2, CHUNK], F32, name="y")
+            nc.vector.tensor_tensor(out=y[:], in0=ya_bank[:], in1=biased[:], op=ALU.max)
             for e in range(2):
                 n = 2 * pair + e
                 nc.vector.tensor_tensor(
-                    pages[n][:].indirect(chunk_of(offs3_t, c)), y[:, e, :], wgo_t[:, c * CHUNK : (c + 1) * CHUNK], ALU.mult
+                    pages[n][:].indirect(entries(offs3_t, c)), y[:, e, :], wgo_t[:, c * CHUNK : (c + 1) * CHUNK], ALU.mult
                 )
                 if c == chunks - 1:
                     nc.sync.dma_start(out[n * P : (n + 1) * P, :], pages[n][:])
 
-        steps = [(0, 0), (1, 0), (0, 1), (1, 1)] + [(c, b) for c in range(2, chunks) for b in range(r_passes)]
-        cosine(0, 0)
+        steps = [(c, b) for b in range(r_passes) for c in range(2)]
+        steps = steps + [(c, b) for c in range(2, chunks) for b in range(r_passes)]
+        views = [(c, pair) for c in range(chunks) for pair in range(n_tiles // 2)]
+
+        cosine(*steps[0])
         quantise_w1(0)
         nc.vector.tensor_scalar(out=neg_gain[:], in0=gain_t[:], scalar1=-1.0, scalar2=None, op0=ALU.mult)
         quantise_w1(1)
-        for c in range(1, chunks):
-            look_up_moods(c)
+        look_up_moods(1)
         look_up_rigs(1)
-        for c, b in steps[1:1]:
-            cosine(c, b)
-        last = len(steps) - 1
-        for step in range(len(steps) + 2):
-            if step + 1 <= last:
-                cosine(*steps[step + 1])
-
-            if step <= last:
+        for step in range(len(views) + LAG):
+            if step < len(steps):
                 c, b = steps[step]
                 features(step, c, b)
-                if b == 1 and c + 2 < chunks:
+                if b == r_passes - 1 and c + 2 < chunks:
+                    look_up_moods(c + 2)
                     look_up_rigs(c + 2)
-            if step == 1:
+            if step == LAG - 1:
                 quantise_w3()
-            if step >= 2:
-                views(step, *divmod(step - 2, 2))
+            if step >= LAG:
+                view(step, *views[step - LAG])
+            if step + 1 < len(steps):
+                cosine(*steps[step + 1])

import math
from contextlib import ExitStack

import concourse.mybir as mybir

K, K2, H, N, T, S, T2 = 1024, 512, 1024, 512, 2048, 1024, 2048
FLOPS = 2 * S * (K * H + K2 * H + 2 * H * N)

F32 = mybir.dt.float32
BF16 = mybir.dt.bfloat16
I32 = mybir.dt.int32
U32 = mybir.dt.uint32
U16 = mybir.dt.uint16
U8 = mybir.dt.uint8
FP8X4 = mybir.dt.float8_e4m3fn_x4
FP4X4 = mybir.dt.float4_e2m1fn_x4
ACT = mybir.ActivationFunctionType
ALU = mybir.AluOpType

P = 128
PACK = 4
PASS = P * PACK
GROUP = 16
QUADRANT = 32
ROWS = 4
CHUNK = 256
LAG = 2


def tile_list_cue_look_proposer_kernel(
    tc, tab_words, tab_scales, tab2_words, tab2_scales, offs, offs2, offs3, w1, w2_words, w2_scales,
    gain, w3, w4_words, w4_scales, b4, page1, wgo, out,
):
    nc = tc.nc
    k_passes = K // PASS
    r_passes = H // PASS
    n_tiles = N // P
    chunks = S // CHUNK
    quadrants = P // QUADRANT

    with ExitStack() as ctx:
        keep = ctx.enter_context(tc.tile_pool(name="keep", bufs=1))
        work = ctx.enter_context(tc.tile_pool(name="work", bufs=2))
        psum = ctx.enter_context(tc.psum_pool(name="psum", bufs=2))

        def held(name, shape, dtype):
            return keep.tile(shape, dtype, name=name, align_bytes=64)

        offs_t = held("offs_t", [P, S // GROUP], U16)
        offs2_t = held("offs2_t", [P, S // GROUP], U16)
        offs3_t = held("offs3_t", [P, S // GROUP], U16)
        tab_w = [held("tab_w%d" % a, [P, T], U32) for a in range(k_passes)]
        tab_s = held("tab_s", [P, T], U8)
        tab2_w = held("tab2_w", [P, T], U32)
        tab2_s = held("tab2_s", [P, T], U8)
        w2_raw = held("w2_raw", [P, 2 * H], U8)
        w2_raw_s = held("w2_raw_s", [P, H], U8)
        w4_w = held("w4_w", [P, r_passes, N], U32)
        w4_s = held("w4_s", [P, r_passes * N], U8)
        w1_raw = [[held("w1_raw%d%d" % (b, a), [P, PACK, PASS], F32) for a in range(k_passes)] for b in range(r_passes)]
        w3_raw = [held("w3_raw%d" % b, [P, PACK, N], F32) for b in range(r_passes)]
        gain_t = held("gain_t", [P, r_passes, PACK], F32)
        b4_t = held("b4_t", [P, n_tiles], F32)
        wgo_t = held("wgo_t", [P, S], F32)
        pages = [held("page%d" % n, [P, T2], F32) for n in range(n_tiles)]

        for scale_tile in (tab_s, w4_s):
            nc.vector.memset(scale_tile[:].bitcast(I32), 0)

        def load_words(tile, dram_words):
            nc.sync.dma_start(tile[:].bitcast(I32), dram_words.rearrange("p c i -> p (c i)").bitcast(I32))

        def load_scales_repeated(scale_tile, rows):
            for d in range(quadrants):
                nc.sync.dma_start(
                    scale_tile[QUADRANT * d : QUADRANT * (d + 1), :].bitcast(I32),
                    rows[ROWS * d : ROWS * (d + 1), :].bitcast(I32).partition_broadcast(QUADRANT // ROWS),
                )

        def load_w4_scales(some_quadrants):
            for d in some_quadrants:
                nc.sync.dma_start(
                    w4_s[QUADRANT * d : QUADRANT * d + ROWS, :].bitcast(I32).rearrange("p (b c) -> p b c", b=r_passes),
                    w4_scales[:, ROWS * d : ROWS * (d + 1), :].bitcast(I32).rearrange("b q c -> q b c"),
                )

        def load_w1(b, a):
            nc.sync.dma_start(
                w1_raw[b][a][:],
                w1[a * PASS : (a + 1) * PASS, b * PASS : (b + 1) * PASS].rearrange("(p j) c -> p j c", j=PACK),
            )

        def entries(list_tile, c):
            return list_tile[:, c * CHUNK // GROUP : (c + 1) * CHUNK // GROUP]

        nc.sync.dma_start(offs2_t[:], offs2)
        load_scales_repeated(tab2_s, tab2_scales[0])
        nc.sync.dma_start(w2_raw[:].bitcast(I32), w2_words[0].bitcast(I32))
        load_words(tab2_w, tab2_words[0])
        nc.sync.dma_start(offs_t[:], offs)
        load_scales_repeated(w2_raw_s, w2_scales[0])
        load_words(tab_w[0], tab_words[0])
        for a in range(k_passes):
            for r in range(2):
                nc.sync.dma_start(tab_s[ROWS * a + r : P : GROUP, :].bitcast(I32), tab_scales[a, r::2, :].bitcast(I32))
        load_words(tab_w[1], tab_words[1])
        nc.sync.dma_start(gain_t[:], gain.rearrange("(b p t) -> p b t", p=P, t=PACK))
        nc.sync.dma_start(offs3_t[:], offs3)
        load_w1(0, 0)
        load_w1(0, 1)
        load_w1(1, 0)
        load_w4_scales(range(quadrants // 2))

        moods = {}
        rigs = {}
        cosines = {}
        h_quantised = {}

        mood_buffers = [
            "mood_words",
            "w2_raw_s",
            "rig_words",
            "w1_raw01",
        ]
        rig_buffers = [
            "rig_words",
            "w1_raw01",
            "gained2",
            "gained3",
        ]

        def look_up_moods(c):
            moods[c] = held(mood_buffers[c], [P, CHUNK], U32)
            nc.vector.tensor_copy(moods[c][:], tab2_w[:].indirect(entries(offs2_t, c)))

        def look_up_rigs(c):
            rigs[c] = held(rig_buffers[c], [P, k_passes, CHUNK], U32)
            for a in range(k_passes):
                nc.vector.tensor_copy(rigs[c][:, a, :], tab_w[a][:].indirect(entries(offs_t, c)))

        mood_s = held("mood_s", [P, S], U8)
        nc.vector.tensor_copy(mood_s[:], tab2_s[:].indirect(offs2_t[:]))
        look_up_moods(0)
        w2_w = held("w2_w", [P, 2 * H], U8)
        w2_s = held("w2_s", [P, H], U8)
        nc.vector.tensor_copy(
            out=w2_w[:].bitcast(U16).rearrange("p (b t m) -> p b m t", b=r_passes, t=PACK),
            in_=w2_raw[:].bitcast(U16).rearrange("p (b m t) -> p b m t", b=r_passes, t=PACK),
        )
        nc.vector.tensor_copy(
            out=w2_s[:].rearrange("p (b t m) -> p b m t", b=r_passes, t=PACK),
            in_=w2_raw_s[:].rearrange("p (b m t) -> p b m t", b=r_passes, t=PACK),
        )

        rig_s_by_list = held("rig_s_by_list", [P, S], U8)
        rig_s = held("rig_s", [P, S], U8)
        nc.vector.tensor_copy(rig_s_by_list[:], tab_s[:].indirect(offs_t[:]))
        nc.vector.tensor_copy(out=rig_s[:].bitcast(I32), in_=rig_s_by_list[:].bitcast(I32))
        for a in range(k_passes):
            for r in range(2):
                nc.sync.dma_start(
                    rig_s[ROWS * a + 2 + r : P : QUADRANT, :].bitcast(I32),
                    rig_s_by_list[GROUP + ROWS * a + r : P : QUADRANT, :].bitcast(I32),
                )

        load_w1(1, 1)
        for b in range(r_passes):
            nc.sync.dma_start(w3_raw[b][:], w3[b * PASS : (b + 1) * PASS, :].rearrange("(p j) c -> p j c", j=PACK))
        load_w4_scales(range(quadrants // 2, quadrants))
        nc.sync.dma_start(w4_w[:].bitcast(I32), w4_words.rearrange("b p c i -> p b (c i)").bitcast(I32))
        nc.sync.dma_start(wgo_t[:], wgo)
        with nc.allow_non_contiguous_dma(reason="one bias value a partition"):
            nc.sync.dma_start(b4_t[:], b4.rearrange("(n p) -> p n", p=P))
        for n in range(n_tiles):
            nc.sync.dma_start(pages[n][:], page1[n * P : (n + 1) * P, :])
        look_up_rigs(0)

        def cosine(c, b):
            cos = work.tile([P, PACK, CHUNK], F32, name="cos", bufs=4)
            for pair in range(PACK // 2):
                bank = psum.tile([P, 2, CHUNK], F32, name="mood_bank")
                for e in range(2):
                    col = b * PASS + (2 * pair + e) * P
                    nc.tensor.matmul_mx(
                        out=bank[:, e, :],
                        lhsT=w2_w[:, 2 * col : 2 * (col + P)].bitcast(FP4X4),
                        lhsT_scale=w2_s[:, col : col + P],
                        rhs=moods[c][:].bitcast(FP8X4),
                        rhs_scale=mood_s[:, c * CHUNK : (c + 1) * CHUNK],
                        start=True,
                        stop=True,
                    )
                nc.scalar.activation(out=cos[:, 2 * pair : 2 * pair + 2, :], in_=bank[:], func=ACT.Abs)
            nc.scalar.activation(out=cos[:], in_=cos[:], func=ACT.Sin, scale=-1.0, bias=math.pi / 2)
            cosines[c, b] = cos

        w1_w = [[held("w1_w%d%d" % (b, a), [P, PASS], U32) for a in range(k_passes)] for b in range(r_passes)]
        w1_s = [[held("w1_s%d%d" % (b, a), [P, PASS], U8) for a in range(k_passes)] for b in range(r_passes)]
        w3_w = [held("w3_w%d" % b, [P, N], U32) for b in range(r_passes)]
        w3_s = [held("w3_s%d" % b, [P, N], U8) for b in range(r_passes)]

        def round_and_quantise(raw_view, pattern, sizes, words, scale_tile):
            rounded = work.tile([P, PACK * PASS], BF16, name="rounded", align_bytes=64, bufs=3)
            nc.vector.tensor_copy(out=rounded[:].rearrange(pattern, **sizes), in_=raw_view)
            nc.vector.quantize_mx(out=words[:].bitcast(FP8X4), scales=scale_tile[:], in_=rounded[:])

        def quantise_w1(b):
            for a in range(k_passes):
                raw_view = w1_raw[b][a][:].rearrange("p j (m t) -> p m j t", t=PACK)
                round_and_quantise(raw_view, "p (t m j) -> p m j t", dict(t=PACK, j=PACK), w1_w[b][a], w1_s[b][a])

        def quantise_w3():
            for b in range(r_passes):
                raw_view = w3_raw[b][:].rearrange("p j (c i) -> p c j i", i=4)
                round_and_quantise(raw_view, "p (c i j) -> p c j i", dict(i=4, j=PACK), w3_w[b], w3_s[b])

        neg_gain = held("neg_gain", [P, r_passes, PACK], F32)

        def scalar_buffer(step, shape):
            return work.tile(shape, F32, name="scalar_buffer%d" % (step % 2), bufs=1)

        def features(step, c, b):
            sine = scalar_buffer(step, [P, PACK, CHUNK])
            for pair in range(PACK // 2):
                bank = psum.tile([P, 2, CHUNK], F32, name="rig_bank")
                for e in range(2):
                    t = 2 * pair + e
                    for a in range(k_passes):
                        nc.tensor.matmul_mx(
                            out=bank[:, e, :],
                            lhsT=w1_w[b][a][:, t * P : (t + 1) * P].bitcast(FP8X4),
                            lhsT_scale=w1_s[b][a][:, t * P : (t + 1) * P],
                            rhs=rigs[c][:, a, :].bitcast(FP8X4),
                            rhs_scale=rig_s[ROWS * a : P, c * CHUNK : (c + 1) * CHUNK],
                            start=(a == 0),
                            stop=(a == k_passes - 1),
                        )
                nc.scalar.activation(
                    out=sine[:, 2 * pair : 2 * pair + 2, :], in_=bank[:], func=ACT.Sin, scale=0.5, bias=-math.pi / 4
                )
            nc.scalar.activation(out=sine[:], in_=sine[:], func=ACT.Square, scale=math.sqrt(2.0))
            gained_name = "gained%d" % step
            if gained_name in rig_buffers:
                gained = held(gained_name, [P, PACK, CHUNK], F32)
            else:
                gained = work.tile([P, PACK, CHUNK], F32, name="gained")
            for t in range(PACK):
                nc.scalar.activation(
                    out=gained[:, t, :], in_=sine[:, t, :], func=ACT.Identity,
                    scale=neg_gain[:, b, t : t + 1], bias=gain_t[:, b, t : t + 1],
                )
            h = work.tile([P, PACK * CHUNK], BF16, name="h", align_bytes=64)
            nc.vector.tensor_tensor(
                out=h[:].rearrange("p (c i t) -> p c t i", i=2, t=PACK),
                in0=gained[:].rearrange("p t (c i) -> p c t i", i=2),
                in1=cosines[c, b][:].rearrange("p t (c i) -> p c t i", i=2),
                op=ALU.mult,
            )
            h_w = work.tile([P, CHUNK], U32, name="h_w", align_bytes=64, bufs=6)
            h_s = work.tile([P, CHUNK], U8, name="h_s", align_bytes=64, bufs=6)
            nc.vector.quantize_mx(out=h_w[:].bitcast(FP8X4), scales=h_s[:], in_=h[:])
            h_quantised[c, b] = (h_w, h_s)

        def second_product(bank, c, pair, words_of, scales_of):
            for e in range(2):
                n = 2 * pair + e
                for b in range(r_passes):
                    h_w, h_s = h_quantised[c, b]
                    nc.tensor.matmul_mx(
                        out=bank[:, e, :],
                        lhsT=words_of(b, n).bitcast(FP8X4),
                        lhsT_scale=scales_of(b, n),
                        rhs=h_w[:].bitcast(FP8X4),
                        rhs_scale=h_s[:],
                        start=(b == 0),
                        stop=(b == r_passes - 1),
                    )

        def view(step, c, pair):
            ya_bank = psum.tile([P, 2, CHUNK], F32, name="ya_bank")
            yb_bank = psum.tile([P, 2, CHUNK], F32, name="yb_bank")
            second_product(
                yb_bank, c, pair,
                lambda b, n: w4_w[:, b, n * P : (n + 1) * P],
                lambda b, n: w4_s[:, b * N + n * P : b * N + (n + 1) * P],
            )
            second_product(
                ya_bank, c, pair,
                lambda b, n: w3_w[b][:, n * P : (n + 1) * P],
                lambda b, n: w3_s[b][:, n * P : (n + 1) * P],
            )
            biased = scalar_buffer(step, [P, 2, CHUNK])
            for e in range(2):
                n = 2 * pair + e
                nc.scalar.activation(out=biased[:, e, :], in_=yb_bank[:, e, :], func=ACT.Identity, bias=b4_t[:, n : n + 1])
            y = work.tile([P, 2, CHUNK], F32, name="y")
            nc.vector.tensor_tensor(out=y[:], in0=ya_bank[:], in1=biased[:], op=ALU.max)
            for e in range(2):
                n = 2 * pair + e
                nc.vector.tensor_tensor(
                    pages[n][:].indirect(entries(offs3_t, c)), y[:, e, :], wgo_t[:, c * CHUNK : (c + 1) * CHUNK], ALU.mult
                )
                if c == chunks - 1:
                    nc.sync.dma_start(out[n * P : (n + 1) * P, :], pages[n][:])

        steps = [(c, b) for b in range(r_passes) for c in range(2)]
        steps = steps + [(c, b) for c in range(2, chunks) for b in range(r_passes)]
        views = [(c, pair) for c in range(chunks) for pair in range(n_tiles // 2)]

        cosine(*steps[0])
        quantise_w1(0)
        nc.vector.tensor_scalar(out=neg_gain[:], in0=gain_t[:], scalar1=-1.0, scalar2=None, op0=ALU.mult)
        quantise_w1(1)
        look_up_moods(1)
        look_up_rigs(1)
        for step in range(len(views) + LAG):
            if step < len(steps):
                c, b = steps[step]
                features(step, c, b)
                if b == r_passes - 1 and c + 2 < chunks:
                    look_up_moods(c + 2)
                    look_up_rigs(c + 2)
            if step == LAG - 1:
                quantise_w3()
            if step >= LAG:
                view(step, *views[step - LAG])
            if step + 1 < len(steps):
                cosine(*steps[step + 1])
